import numpy as np
import ml_dtypes


def mxq(x, axis, fmt="e4m3"):
    dtype, down = {"e4m3": (ml_dtypes.float8_e4m3fn, 7), "e5m2": (ml_dtypes.float8_e5m2, 14)}[fmt]
    v = np.moveaxis(np.asarray(x, np.float32).astype(ml_dtypes.bfloat16).astype(np.float64), axis, -1)
    blocks = v.reshape(v.shape[:-1] + (-1, 32))
    amax = np.abs(blocks).max(-1, keepdims=True)
    byte = np.maximum(np.where(amax > 0, np.frexp(amax)[1] - 1 + 127, 0) - down, 1)
    scale = np.exp2(byte - 127.0)
    codes = (blocks / scale).astype(np.float32).astype(dtype).astype(np.float64)
    return np.moveaxis((codes * scale).reshape(v.shape), -1, axis)


WIDE = False


def mx_kscale(k):
    if not WIDE:
        return np.ones(k)
    levels = np.array([10, -10, 5, -5, 0])
    if k % 512:
        return np.exp2(np.random.permutation(np.resize(levels, k // 32))).repeat(32)
    a = np.empty((k // 512, 16))
    for p in range(k // 512):
        a[p, :8] = np.random.permutation(np.resize(levels, 8))
        for g in range(8):
            far = levels[np.abs(levels - a[p, g]) >= 10]
            a[p, g + 8] = far[np.random.randint(len(far))]
    return np.exp2(a.ravel()).repeat(32)


def f64(x):
    return np.asarray(x).astype(np.float64)


def striped(idx):
    return np.tile(idx.reshape(-1, 16).T, (8, 1)).astype(np.uint16)


def unstriped(offs):
    return offs[:16].T.reshape(-1).astype(np.int64)


E2M1 = np.array([0.0, 0.5, 1.0, 1.5, 2.0, 3.0, 4.0, 6.0, -0.0, -0.5, -1.0, -1.5, -2.0, -3.0, -4.0, -6.0])


def pack_weight(w, fmt):
    k, n = w.shape
    w = f64(np.asarray(w, np.float32).astype(ml_dtypes.bfloat16)).reshape(k // 32, 32, n)
    amax = np.abs(w).max(1)
    if fmt == "e4m3":
        byte = np.frexp(amax)[1] - 1 + 127 - 7
    else:
        mant, ex = np.frexp(amax / 6.0)
        byte = np.where(mant > 0.5, ex, ex - 1) + 127
    byte = np.clip(np.where(amax > 0, byte, 1), 1, 254)
    scaled = (w * np.exp2(127.0 - byte)[:, None, :]).reshape(k, n).astype(np.float32)
    by_word = np.ascontiguousarray(scaled.reshape(k // 512, 128, 4, n).transpose(0, 1, 3, 2))
    if fmt == "e4m3":
        words = by_word.astype(ml_dtypes.float8_e4m3fn).view(np.uint8)
    else:
        c = by_word.astype(ml_dtypes.float4_e2m1fn).view(np.uint8) & 0xF
        words = (c[..., 0::2] | (c[..., 1::2] << 4)).reshape(k // 512, 128, 2 * n)
    return np.ascontiguousarray(words), np.ascontiguousarray(byte.astype(np.uint8).reshape(k // 512, 16, n))


def unpack_weight(words, scales, fmt):
    g, _, n = scales.shape
    words = np.ascontiguousarray(words).reshape(g, 128, n, -1)
    if fmt == "e4m3":
        vals = words.view(ml_dtypes.float8_e4m3fn).astype(np.float64)
    else:
        nib = np.empty((g, 128, n, 4), np.uint8)
        nib[..., 0::2] = words & 0xF
        nib[..., 1::2] = words >> 4
        vals = E2M1[nib]
    vals = vals * np.repeat(np.exp2(scales.astype(np.float64) - 127.0), 8, axis=1)[..., None]
    return vals.transpose(0, 1, 3, 2).reshape(g * 512, n)


def gelu(v):
    return 0.5 * v * (1.0 + np.tanh(np.sqrt(2.0 / np.pi) * (v + 0.044715 * v**3)))


def striped8(idx):
    return np.concatenate([v.reshape(-1, 16).T for v in idx]).astype(np.uint16)


def unstriped8(offs):
    return np.stack([offs[16 * g:16 * g + 16].T.reshape(-1) for g in range(8)]).astype(np.int64)


def heads(h, wgt, idx8):
    r = np.arange(h.shape[0])
    return wgt[r // 4 % 128] * h[r[:, None], idx8[r % 512 // 64]]


def put_heads(h, wgs, idx8, t2):
    r = np.arange(h.shape[0])
    page = np.zeros((h.shape[0], t2))
    page[r[:, None], idx8[r % 512 // 64]] = wgs[r // 4 % 128] * h
    return page


K, H, N, T, S, P, T2 = 1536, 1024, 1024, 4096, 1024, 512, 1024

def setup_inputs():
    n = np.random.standard_normal
    s = mx_kscale(K)[:, None]
    u = mx_kscale(H)[:, None]
    d = {}
    d["tab_words"], d["tab_scales"] = pack_weight(n((K, T)) * s, "e4m3")
    d["w1"] = (1.5 * n((K, H)) / s / K**0.5).astype(np.float32)
    d["w4_words"], d["w4_scales"] = pack_weight(1.6 * n((H, N)) / u / H**0.5, "e2m1")
    d["gain"] = np.random.uniform(0.6, 1.1, H).astype(np.float32)
    d["shift"] = np.random.uniform(-0.7, 0.7, H).astype(np.float32)
    d["amp"] = (np.exp(0.3 * n(H)) * u[:, 0]).astype(np.float32)
    d["wgt"] = np.repeat(np.random.uniform(0.5, 2.0, (8, P)), 16, axis=0).astype(np.float32)
    d["wgo"] = np.repeat(np.random.uniform(0.5, 2.0, (8, P)), 16, axis=0).astype(np.float32)
    d["offs"] = striped(np.random.permutation(T)[:S])
    d["offs2"] = striped8(np.stack([np.random.permutation(S)[:P] for _ in range(8)]))
    d["offs3"] = striped8(np.stack([np.random.permutation(T2)[:P] for _ in range(8)]))
    return d

def reference(tab_words, tab_scales, w1, w4_words, w4_scales, gain, shift, amp, wgt, wgo, offs, offs2, offs3):
    v = unpack_weight(tab_words, tab_scales, "e4m3")[:, unstriped(offs)]
    h = f64(gain)[:, None] * np.tanh(mxq(f64(w1), 0, "e4m3").T @ v)
    x = heads(h, f64(wgt), unstriped8(offs2))
    z = f64(amp)[:, None] * np.sin(x + f64(shift)[:, None])
    w4 = unpack_weight(w4_words, w4_scales, "e2m1")
    y = np.abs(w4.T @ mxq(z, 0, "e4m3"))
    return put_heads(y, f64(wgo), unstriped8(offs3), T2)

@@ -1,0 +1,235 @@
+from contextlib import ExitStack
+
+import concourse.mybir as mybir
+
+K, H, N, T, S, M, T2 = 1536, 1024, 1024, 4096, 1024, 512, 1024
+FLOPS = 2 * K * H * S + 2 * H * N * M
+
+F32 = mybir.dt.float32
+BF16 = mybir.dt.bfloat16
+I32 = mybir.dt.int32
+U32 = mybir.dt.uint32
+U16 = mybir.dt.uint16
+U8 = mybir.dt.uint8
+FP8X4 = mybir.dt.float8_e4m3fn_x4
+FP4X4 = mybir.dt.float4_e2m1fn_x4
+ACT = mybir.ActivationFunctionType
+MULT = mybir.AluOpType.mult
+
+P = 128
+BANK = 512
+PASSES1 = K // 512
+BLOCKS = H // 512
+PAGES = 4
+
+
+def tile_list_larval_panel_scores_kernel(
+    tc, tab_words, tab_scales, w1, w4_words, w4_scales, gain, shift, amp, wgt, wgo, offs, offs2, offs3, out
+):
+    nc = tc.nc
+    with ExitStack() as ctx:
+        keep = ctx.enter_context(tc.tile_pool(name="keep", bufs=1))
+        ring = ctx.enter_context(tc.tile_pool(name="ring", bufs=1))
+        psum = ctx.enter_context(tc.psum_pool(name="psum", bufs=1))
+
+        list1 = keep.tile([P, S // 16], U16, name="list1")
+        list2 = keep.tile([P, M // 16], U16, name="list2")
+        list3 = keep.tile([P, M // 16], U16, name="list3")
+        tab_w = [keep.tile([P, T], I32, name="tab_w%d" % a) for a in range(PASSES1)]
+        tab_s = keep.tile([P, T], U8, name="tab_s")
+        v_w = [keep.tile([P, S], U32, name="v_w%d" % a, align_bytes=64) for a in range(PASSES1)]
+        v_s = keep.tile([P, S], U8, name="v_s", align_bytes=64)
+        w1_raw = {}
+        w1_w = {}
+        w1_s = {}
+        for b in range(BLOCKS):
+            for a in range(PASSES1):
+                w1_raw[b, a] = keep.tile([P, 4, 512], F32, name="w1_raw%d%d" % (b, a))
+                w1_w[b, a] = keep.tile([P, 512], U32, name="w1_w%d%d" % (b, a), align_bytes=64)
+                w1_s[b, a] = keep.tile([P, 512], U8, name="w1_s%d%d" % (b, a), align_bytes=64)
+        w4_raw_w = keep.tile([P, BLOCKS, 2 * N], U8, name="w4_raw_w")
+        w4_raw_s = keep.tile([P, BLOCKS, N], U8, name="w4_raw_s")
+        w4_w = keep.tile([P, BLOCKS, 2 * N], U8, name="w4_w", align_bytes=64)
+        w4_s = keep.tile([P, BLOCKS, N], U8, name="w4_s", align_bytes=64)
+        gain_t = keep.tile([P, BLOCKS, 4], F32, name="gain_t")
+        shift_t = keep.tile([P, BLOCKS, 4], F32, name="shift_t")
+        amp_t = keep.tile([P, BLOCKS, 4], F32, name="amp_t")
+        wgt_t = keep.tile([P, M], F32, name="wgt_t")
+        wgo_t = keep.tile([P, M], F32, name="wgo_t")
+        pages = [keep.tile([P, T2], F32, name="page%d" % i) for i in range(PAGES)]
+        z_w = [keep.tile([P, M], U32, name="z_w%d" % b, align_bytes=64) for b in range(BLOCKS)]
+        z_s = [keep.tile([P, M], U8, name="z_s%d" % b, align_bytes=64) for b in range(BLOCKS)]
+
+        def load_w1(b, a):
+            rows = w1[512 * a : 512 * (a + 1), 512 * b : 512 * (b + 1)]
+            nc.sync.dma_start(out=w1_raw[b, a][:], in_=rows.rearrange("(p j) c -> p j c", j=4))
+
+        def load_table(a):
+            nc.sync.dma_start(out=tab_w[a][:], in_=tab_words[a].rearrange("p t i -> p (t i)").bitcast(I32))
+
+        def load_rows(dst, vec):
+            nc.sync.dma_start(out=dst[:], in_=vec.rearrange("(b p i) -> p b i", b=BLOCKS, i=4))
+
+        warm = keep.tile([P, 2], F32, name="warm")
+        nc.vector.memset(warm[:], 0.0)
+        nc.scalar.activation(out=warm[:, 1:2], in_=warm[:, 0:1], func=ACT.Silu)
+        nc.vector.memset(tab_s[:].bitcast(I32), 0)
+        nc.vector.memset(w4_raw_s[:].bitcast(I32), 0)
+        for page in pages:
+            nc.vector.memset(page[:], 0.0)
+
+        nc.sync.dma_start(list1[:], offs)
+        load_rows(gain_t, gain)
+        load_rows(shift_t, shift)
+        load_rows(amp_t, amp)
+        nc.sync.dma_start(list2[:], offs2)
+        nc.sync.dma_start(list3[:], offs3)
+        load_w1(0, 0)
+        load_table(0)
+        for q in range(4):
+            nc.scalar.dma_start(
+                out=tab_s[32 * q : 32 * q + 4 * PASSES1, :].bitcast(I32),
+                in_=tab_scales[:, 4 * q : 4 * q + 4, :].bitcast(I32),
+            )
+        load_w1(0, 1)
+        nc.sync.dma_start(out=w4_raw_w[:].bitcast(I32), in_=w4_words.rearrange("a p n -> p a n").bitcast(I32))
+        load_table(1)
+        for q in range(4):
+            nc.sync.dma_start(
+                out=w4_raw_s[32 * q : 32 * q + 4, :, :].bitcast(I32),
+                in_=w4_scales[:, 4 * q : 4 * q + 4, :].rearrange("a r n -> r a n").bitcast(I32),
+            )
+        load_w1(0, 2)
+        load_table(2)
+        nc.sync.dma_start(out=wgt_t[:], in_=wgt)
+        for a in range(PASSES1):
+            load_w1(1, a)
+        nc.sync.dma_start(out=wgo_t[:], in_=wgo)
+
+        def cast_w1(b, a, on_vector):
+            grouped = ring.tile([P, 2048], BF16, name="grouped", tag="grouped", bufs=3, align_bytes=64)
+            dst = grouped[:].rearrange("p (t m j) -> p m j t", t=4, j=4)
+            src = w1_raw[b, a][:].rearrange("p j (m t) -> p m j t", t=4)
+            if on_vector:
+                nc.vector.tensor_copy(out=dst, in_=src)
+            else:
+                nc.scalar.copy(out=dst, in_=src)
+            nc.vector.quantize_mx(out=w1_w[b, a][:].bitcast(FP8X4), scales=w1_s[b, a][:], in_=grouped[:])
+
+        def gather_words(a, lo, hi):
+            window = tab_w[a][:].bitcast(U32)
+            nc.vector.tensor_copy(out=v_w[a][:, lo:hi], in_=window.indirect(list1[:, lo // 16 : hi // 16]))
+
+        def new_bank(i):
+            return psum.tile([P, BANK], F32, name="bank%d" % i, tag="bank%d" % i)
+
+        def first_product(bank, b, t, half, a):
+            cols = slice(128 * t, 128 * (t + 1))
+            picks = slice(BANK * half, BANK * (half + 1))
+            nc.tensor.matmul_mx(
+                out=bank[:],
+                lhsT=w1_w[b, a][:, cols].bitcast(FP8X4),
+                lhsT_scale=w1_s[b, a][:, cols],
+                rhs=v_w[a][:, picks].bitcast(FP8X4),
+                rhs_scale=v_s[4 * a : P, picks],
+                start=(a == 0),
+                stop=(a == PASSES1 - 1),
+            )
+
+        def read_panels(banks2):
+            h = ring.tile([P, S], F32, name="h", tag="h", bufs=4)
+            for half in range(2):
+                nc.scalar.activation(out=h[:, BANK * half : BANK * (half + 1)], in_=banks2[half][:], func=ACT.Tanh)
+            x = ring.tile([P, M], F32, name="x", tag="x", bufs=8)
+            nc.vector.tensor_tensor(x[:], h[:].indirect(list2[:]), wgt_t[:], MULT)
+            return x
+
+        def respond(x, z_rows, b, t):
+            s = ring.tile([P, M], F32, name="s", tag="s", bufs=3)
+            nc.scalar.activation(
+                out=s[:], in_=x[:], func=ACT.Sin, bias=shift_t[:, b, t : t + 1], scale=gain_t[:, b, t : t + 1]
+            )
+            if b == 0:
+                nc.scalar.activation(out=z_rows[:, t, :], in_=s[:], func=ACT.Copy, scale=amp_t[:, b, t : t + 1])
+            else:
+                nc.vector.tensor_scalar(z_rows[:, t, :], s[:], amp_t[:, b, t : t + 1], None, MULT)
+
+        def quantize_z(z_rows, b):
+            grouped = ring.tile([P, 2048], BF16, name="grouped", tag="grouped", bufs=3, align_bytes=64)
+            nc.vector.tensor_copy(
+                out=grouped[:].rearrange("p (c e t) -> p c t e", e=4, t=4),
+                in_=z_rows[:].rearrange("p t (c e) -> p c t e", e=4),
+            )
+            nc.vector.quantize_mx(out=z_w[b][:].bitcast(FP8X4), scales=z_s[b][:], in_=grouped[:])
+
+        cast_w1(0, 0, False)
+        nc.vector.tensor_copy(out=v_s[:], in_=tab_s[:].indirect(list1[:]))
+        gather_words(0, 0, S)
+        banks = [new_bank(i) for i in range(8)]
+        for t in range(4):
+            for half in range(2):
+                first_product(banks[2 * t + half], 0, t, half, 0)
+        cast_w1(0, 1, False)
+        nc.vector.tensor_copy(
+            out=w4_w[:].rearrange("p a (b t q e) -> p (a b) t q e", b=2, t=4, e=2),
+            in_=w4_raw_w[:].rearrange("p a (b q t e) -> p (a b) t q e", b=2, t=4, e=2),
+        )
+        nc.vector.tensor_copy(
+            out=w4_s[:].rearrange("p a (b t q) -> p (a b) t q", b=2, t=4),
+            in_=w4_raw_s[:].rearrange("p a (b q t) -> p (a b) t q", b=2, t=4),
+        )
+        gather_words(1, 0, S)
+        for t in range(4):
+            for half in range(2):
+                first_product(banks[2 * t + half], 0, t, half, 1)
+        cast_w1(0, 2, False)
+        gather_words(2, 0, BANK)
+        gather_words(2, BANK, S)
+        xs = {}
+        for t in range(4):
+            for half in range(2):
+                first_product(banks[2 * t + half], 0, t, half, 2)
+            xs[0, t] = read_panels(banks[2 * t : 2 * t + 2])
+        cast_w1(1, 0, False)
+        cast_w1(1, 1, False)
+        cast_w1(1, 2, True)
+        z_rows = [ring.tile([P, 4, M], BF16, name="z_rows%d" % b, tag="z_rows", bufs=2) for b in range(BLOCKS)]
+        banks = [new_bank(i) for i in range(8)]
+        for a in range(PASSES1 - 1):
+            for t in range(4):
+                for half in range(2):
+                    first_product(banks[2 * t + half], 1, t, half, a)
+        respond(xs[0, 0], z_rows[0], 0, 0)
+        respond(xs[0, 1], z_rows[0], 0, 1)
+        for t in range(4):
+            for half in range(2):
+                first_product(banks[2 * t + half], 1, t, half, 2)
+            xs[1, t] = read_panels(banks[2 * t : 2 * t + 2])
+            if t < 2:
+                respond(xs[0, t + 2], z_rows[0], 0, t + 2)
+        for t in range(3):
+            respond(xs[1, t], z_rows[1], 1, t)
+        quantize_z(z_rows[0], 0)
+        respond(xs[1, 3], z_rows[1], 1, 3)
+        quantize_z(z_rows[1], 1)
+
+        out_rows = out.rearrange("(b p t) c -> b t p c", p=P, t=4)
+        for b in range(BLOCKS):
+            for t in range(4):
+                i = 4 * b + t
+                bank = new_bank(i)
+                for a in range(BLOCKS):
+                    nc.tensor.matmul_mx(
+                        out=bank[:],
+                        lhsT=w4_w[:, a, 256 * i : 256 * (i + 1)].bitcast(FP4X4),
+                        lhsT_scale=w4_s[:, a, 128 * i : 128 * (i + 1)],
+                        rhs=z_w[a][:].bitcast(FP8X4),
+                        rhs_scale=z_s[a][:],
+                        start=(a == 0),
+                        stop=(a == BLOCKS - 1),
+                    )
+                y = ring.tile([P, M], F32, name="y", tag="y", bufs=3)
+                nc.scalar.activation(out=y[:], in_=bank[:], func=ACT.Abs)
+                page = pages[i % PAGES]
+                nc.vector.tensor_tensor(page[:].indirect(list3[:]), y[:], wgo_t[:], MULT)
+                nc.sync.dma_start(out=out_rows[b, t], in_=page[:])

@@ -20,7 +20,8 @@ P = 128
 BANK = 512
 PASSES1 = K // 512
 BLOCKS = H // 512
-PAGES = 4
+PAGES = 8
+HALF = M // 2
 
 
 def tile_list_larval_panel_scores_kernel(
@@ -44,11 +45,12 @@ def tile_list_larval_panel_scores_kernel(
         w1_s = {}
         for b in range(BLOCKS):
             for a in range(PASSES1):
-                w1_raw[b, a] = keep.tile([P, 4, 512], F32, name="w1_raw%d%d" % (b, a))
+                w1_raw[b, a] = ring.tile([P, 4, 512], F32, name="w1_raw", tag="w1_raw", bufs=5)
                 w1_w[b, a] = keep.tile([P, 512], U32, name="w1_w%d%d" % (b, a), align_bytes=64)
                 w1_s[b, a] = keep.tile([P, 512], U8, name="w1_s%d%d" % (b, a), align_bytes=64)
         w4_raw_w = keep.tile([P, BLOCKS, 2 * N], U8, name="w4_raw_w")
-        w4_raw_s = keep.tile([P, BLOCKS, N], U8, name="w4_raw_s")
+        w4_raw_s = keep.tile([P, N], U8, name="w4_raw_s")
+        w4_dealt_s = keep.tile([P, N], U8, name="w4_dealt_s")
         w4_w = keep.tile([P, BLOCKS, 2 * N], U8, name="w4_w", align_bytes=64)
         w4_s = keep.tile([P, BLOCKS, N], U8, name="w4_s", align_bytes=64)
         gain_t = keep.tile([P, BLOCKS, 4], F32, name="gain_t")
@@ -75,46 +77,62 @@ def tile_list_larval_panel_scores_kernel(
         nc.scalar.activation(out=warm[:, 1:2], in_=warm[:, 0:1], func=ACT.Silu)
         nc.vector.memset(tab_s[:].bitcast(I32), 0)
         nc.vector.memset(w4_raw_s[:].bitcast(I32), 0)
+        nc.vector.memset(w4_s[:].bitcast(I32), 0)
         for page in pages:
             nc.vector.memset(page[:], 0.0)
 
         nc.sync.dma_start(list1[:], offs)
-        load_rows(gain_t, gain)
-        load_rows(shift_t, shift)
-        load_rows(amp_t, amp)
-        nc.sync.dma_start(list2[:], offs2)
-        nc.sync.dma_start(list3[:], offs3)
-        load_w1(0, 0)
         load_table(0)
         for q in range(4):
-            nc.scalar.dma_start(
+            nc.sync.dma_start(
                 out=tab_s[32 * q : 32 * q + 4 * PASSES1, :].bitcast(I32),
                 in_=tab_scales[:, 4 * q : 4 * q + 4, :].bitcast(I32),
             )
+        load_w1(0, 0)
+        nc.sync.dma_start(
+            out=w4_raw_s[0:32, :].bitcast(I32), in_=w4_scales.rearrange("a q n -> (a q) n").bitcast(I32)
+        )
         load_w1(0, 1)
-        nc.sync.dma_start(out=w4_raw_w[:].bitcast(I32), in_=w4_words.rearrange("a p n -> p a n").bitcast(I32))
         load_table(1)
-        for q in range(4):
-            nc.sync.dma_start(
-                out=w4_raw_s[32 * q : 32 * q + 4, :, :].bitcast(I32),
-                in_=w4_scales[:, 4 * q : 4 * q + 4, :].rearrange("a r n -> r a n").bitcast(I32),
-            )
-        load_w1(0, 2)
         load_table(2)
+        load_w1(0, 2)
+        nc.sync.dma_start(out=w4_raw_w[:].bitcast(I32), in_=w4_words.rearrange("a p n -> p a n").bitcast(I32))
         nc.sync.dma_start(out=wgt_t[:], in_=wgt)
-        for a in range(PASSES1):
-            load_w1(1, a)
+        nc.sync.dma_start(list2[:], offs2)
+        load_w1(1, 0)
+        load_w1(1, 1)
+        load_w1(1, 2)
+        load_rows(gain_t, gain)
+        load_rows(shift_t, shift)
+        load_rows(amp_t, amp)
+        nc.sync.dma_start(list3[:], offs3)
         nc.sync.dma_start(out=wgo_t[:], in_=wgo)
 
-        def cast_w1(b, a, on_vector):
-            grouped = ring.tile([P, 2048], BF16, name="grouped", tag="grouped", bufs=3, align_bytes=64)
-            dst = grouped[:].rearrange("p (t m j) -> p m j t", t=4, j=4)
-            src = w1_raw[b, a][:].rearrange("p j (m t) -> p m j t", t=4)
+        def copy_on(on_vector, dst, src):
             if on_vector:
                 nc.vector.tensor_copy(out=dst, in_=src)
             else:
                 nc.scalar.copy(out=dst, in_=src)
+
+        def cast_w1(b, a, on_vector):
+            grouped = ring.tile([P, 2048], BF16, name="grouped", tag="grouped", bufs=2, align_bytes=64)
+            dst = grouped[:].rearrange("p (t m j) -> p m j t", t=4, j=4)
+            copy_on(on_vector, dst, w1_raw[b, a][:].rearrange("p j (m t) -> p m j t", t=4))
+            return grouped
+
+        def quantize_w1(b, a, grouped):
             nc.vector.quantize_mx(out=w1_w[b, a][:].bitcast(FP8X4), scales=w1_s[b, a][:], in_=grouped[:])
+
+        def cast_w1_half(b, a, u, on_vector):
+            grouped = ring.tile([P, 1024], BF16, name="grouped_half", tag="grouped_half", bufs=3, align_bytes=64)
+            dst = grouped[:].rearrange("p (t m j) -> p m j t", t=2, j=4)
+            src = w1_raw[b, a][:].rearrange("p j (m t) -> p m j t", t=4)
+            copy_on(on_vector, dst, src[:, :, :, 2 * u : 2 * u + 2])
+            return grouped
+
+        def quantize_w1_half(b, a, u, grouped):
+            cols = slice(256 * u, 256 * (u + 1))
+            nc.vector.quantize_mx(out=w1_w[b, a][:, cols].bitcast(FP8X4), scales=w1_s[b, a][:, cols], in_=grouped[:])
 
         def gather_words(a, lo, hi):
             window = tab_w[a][:].bitcast(U32)
@@ -123,7 +141,7 @@ def tile_list_larval_panel_scores_kernel(
         def new_bank(i):
             return psum.tile([P, BANK], F32, name="bank%d" % i, tag="bank%d" % i)
 
-        def first_product(bank, b, t, half, a):
+        def first_product(bank, b, t, half, a, order):
             cols = slice(128 * t, 128 * (t + 1))
             picks = slice(BANK * half, BANK * (half + 1))
             nc.tensor.matmul_mx(
@@ -132,104 +150,166 @@ def tile_list_larval_panel_scores_kernel(
                 lhsT_scale=w1_s[b, a][:, cols],
                 rhs=v_w[a][:, picks].bitcast(FP8X4),
                 rhs_scale=v_s[4 * a : P, picks],
-                start=(a == 0),
-                stop=(a == PASSES1 - 1),
+                start=(a == order[0]),
+                stop=(a == order[-1]),
             )
 
-        def read_panels(banks2):
+        def both_halves(banks, b, t, a):
+            for half in range(2):
+                first_product(banks[2 * t + half], b, t, half, a, (0, 1, 2))
+
+        hs = {}
+        xs = {}
+        z_rows = {}
+        for b in range(BLOCKS):
+            for u in range(2):
+                z_rows[b, u] = keep.tile([P, 4, HALF], BF16, name="z_rows%d%d" % (b, u))
+            for t in range(4):
+                xs[b, t] = keep.tile([P, M], F32, name="x%d%d" % (b, t))
+
+        def traits(banks, b, t):
             h = ring.tile([P, S], F32, name="h", tag="h", bufs=4)
             for half in range(2):
-                nc.scalar.activation(out=h[:, BANK * half : BANK * (half + 1)], in_=banks2[half][:], func=ACT.Tanh)
-            x = ring.tile([P, M], F32, name="x", tag="x", bufs=8)
-            nc.vector.tensor_tensor(x[:], h[:].indirect(list2[:]), wgt_t[:], MULT)
-            return x
+                nc.scalar.activation(
+                    out=h[:, BANK * half : BANK * (half + 1)], in_=banks[2 * t + half][:], func=ACT.Tanh
+                )
+            hs[b, t] = h
 
-        def respond(x, z_rows, b, t):
-            s = ring.tile([P, M], F32, name="s", tag="s", bufs=3)
+        def read_panels(b, t, lo, hi):
+            window = hs[b, t][:].indirect(list2[:, lo // 16 : hi // 16])
+            nc.vector.tensor_tensor(xs[b, t][:, lo:hi], window, wgt_t[:, lo:hi], MULT)
+
+        def respond(b, t, u, on_vector):
+            s = ring.tile([P, HALF], F32, name="s", tag="s", bufs=3)
             nc.scalar.activation(
-                out=s[:], in_=x[:], func=ACT.Sin, bias=shift_t[:, b, t : t + 1], scale=gain_t[:, b, t : t + 1]
+                out=s[:],
+                in_=xs[b, t][:, HALF * u : HALF * (u + 1)],
+                func=ACT.Sin,
+                bias=shift_t[:, b, t : t + 1],
+                scale=gain_t[:, b, t : t + 1],
             )
-            if b == 0:
-                nc.scalar.activation(out=z_rows[:, t, :], in_=s[:], func=ACT.Copy, scale=amp_t[:, b, t : t + 1])
+            if on_vector:
+                nc.vector.tensor_scalar(z_rows[b, u][:, t, :], s[:], amp_t[:, b, t : t + 1], None, MULT)
             else:
-                nc.vector.tensor_scalar(z_rows[:, t, :], s[:], amp_t[:, b, t : t + 1], None, MULT)
+                nc.scalar.activation(out=z_rows[b, u][:, t, :], in_=s[:], func=ACT.Copy, scale=amp_t[:, b, t : t + 1])
 
-        def quantize_z(z_rows, b):
-            grouped = ring.tile([P, 2048], BF16, name="grouped", tag="grouped", bufs=3, align_bytes=64)
-            nc.vector.tensor_copy(
-                out=grouped[:].rearrange("p (c e t) -> p c t e", e=4, t=4),
-                in_=z_rows[:].rearrange("p t (c e) -> p c t e", e=4),
+        def quantize_z(b, u, on_vector):
+            grouped = ring.tile([P, 1024], BF16, name="grouped_half", tag="grouped_half", bufs=3, align_bytes=64)
+            copy_on(
+                on_vector,
+                grouped[:].rearrange("p (c e t) -> p c t e", e=4, t=4),
+                z_rows[b, u][:].rearrange("p t (c e) -> p c t e", e=4),
             )
-            nc.vector.quantize_mx(out=z_w[b][:].bitcast(FP8X4), scales=z_s[b][:], in_=grouped[:])
-
-        cast_w1(0, 0, False)
-        nc.vector.tensor_copy(out=v_s[:], in_=tab_s[:].indirect(list1[:]))
-        gather_words(0, 0, S)
-        banks = [new_bank(i) for i in range(8)]
-        for t in range(4):
-            for half in range(2):
-                first_product(banks[2 * t + half], 0, t, half, 0)
-        cast_w1(0, 1, False)
-        nc.vector.tensor_copy(
-            out=w4_w[:].rearrange("p a (b t q e) -> p (a b) t q e", b=2, t=4, e=2),
-            in_=w4_raw_w[:].rearrange("p a (b q t e) -> p (a b) t q e", b=2, t=4, e=2),
-        )
-        nc.vector.tensor_copy(
-            out=w4_s[:].rearrange("p a (b t q) -> p (a b) t q", b=2, t=4),
-            in_=w4_raw_s[:].rearrange("p a (b q t) -> p (a b) t q", b=2, t=4),
-        )
-        gather_words(1, 0, S)
-        for t in range(4):
-            for half in range(2):
-                first_product(banks[2 * t + half], 0, t, half, 1)
-        cast_w1(0, 2, False)
-        gather_words(2, 0, BANK)
-        gather_words(2, BANK, S)
-        xs = {}
-        for t in range(4):
-            for half in range(2):
-                first_product(banks[2 * t + half], 0, t, half, 2)
-            xs[0, t] = read_panels(banks[2 * t : 2 * t + 2])
-        cast_w1(1, 0, False)
-        cast_w1(1, 1, False)
-        cast_w1(1, 2, True)
-        z_rows = [ring.tile([P, 4, M], BF16, name="z_rows%d" % b, tag="z_rows", bufs=2) for b in range(BLOCKS)]
-        banks = [new_bank(i) for i in range(8)]
-        for a in range(PASSES1 - 1):
-            for t in range(4):
-                for half in range(2):
-                    first_product(banks[2 * t + half], 1, t, half, a)
-        respond(xs[0, 0], z_rows[0], 0, 0)
-        respond(xs[0, 1], z_rows[0], 0, 1)
-        for t in range(4):
-            for half in range(2):
-                first_product(banks[2 * t + half], 1, t, half, 2)
-            xs[1, t] = read_panels(banks[2 * t : 2 * t + 2])
-            if t < 2:
-                respond(xs[0, t + 2], z_rows[0], 0, t + 2)
-        for t in range(3):
-            respond(xs[1, t], z_rows[1], 1, t)
-        quantize_z(z_rows[0], 0)
-        respond(xs[1, 3], z_rows[1], 1, 3)
-        quantize_z(z_rows[1], 1)
+            cols = slice(HALF * u, HALF * (u + 1))
+            nc.vector.quantize_mx(out=z_w[b][:, cols].bitcast(FP8X4), scales=z_s[b][:, cols], in_=grouped[:])
 
         out_rows = out.rearrange("(b p t) c -> b t p c", p=P, t=4)
-        for b in range(BLOCKS):
-            for t in range(4):
-                i = 4 * b + t
-                bank = new_bank(i)
+
+        def second_product(i, u):
+            bank = new_bank(i)
+            for g in range(HALF // 128):
+                cols = slice(HALF * u + 128 * g, HALF * u + 128 * (g + 1))
                 for a in range(BLOCKS):
                     nc.tensor.matmul_mx(
-                        out=bank[:],
+                        out=bank[:, 128 * g : 128 * (g + 1)],
                         lhsT=w4_w[:, a, 256 * i : 256 * (i + 1)].bitcast(FP4X4),
                         lhsT_scale=w4_s[:, a, 128 * i : 128 * (i + 1)],
-                        rhs=z_w[a][:].bitcast(FP8X4),
-                        rhs_scale=z_s[a][:],
+                        rhs=z_w[a][:, cols].bitcast(FP8X4),
+                        rhs_scale=z_s[a][:, cols],
                         start=(a == 0),
                         stop=(a == BLOCKS - 1),
                     )
-                y = ring.tile([P, M], F32, name="y", tag="y", bufs=3)
-                nc.scalar.activation(out=y[:], in_=bank[:], func=ACT.Abs)
-                page = pages[i % PAGES]
-                nc.vector.tensor_tensor(page[:].indirect(list3[:]), y[:], wgo_t[:], MULT)
-                nc.sync.dma_start(out=out_rows[b, t], in_=page[:])
+            return bank
+
+        def put_scores(bank, i, u):
+            y = ring.tile([P, HALF], F32, name="y", tag="y", bufs=4)
+            nc.scalar.activation(out=y[:], in_=bank[:, 0:HALF], func=ACT.Abs)
+            cols = slice(HALF * u, HALF * (u + 1))
+            slots = pages[i][:].indirect(list3[:, HALF * u // 16 : HALF * (u + 1) // 16])
+            nc.vector.tensor_tensor(slots, y[:], wgo_t[:, cols], MULT)
+
+        gather_words(0, 0, S)
+        nc.vector.tensor_copy(out=v_s[:], in_=tab_s[:].indirect(list1[:]))
+        quantize_w1(0, 0, cast_w1(0, 0, False))
+        banks0 = [new_bank(i) for i in range(8)]
+        for t in range(4):
+            both_halves(banks0, 0, t, 0)
+        nc.vector.tensor_copy(
+            out=w4_dealt_s[:].rearrange("p (b t q) -> p b t q", b=2, t=4),
+            in_=w4_raw_s[:].rearrange("p (b q t) -> p b t q", b=2, t=4),
+        )
+        quantize_w1(0, 1, cast_w1(0, 1, False))
+        gather_words(1, 0, S)
+        for t in range(4):
+            both_halves(banks0, 0, t, 1)
+        gather_words(2, 0, S)
+        halves = [cast_w1_half(0, 2, u, u == 0) for u in range(2)]
+        for u in range(2):
+            quantize_w1_half(0, 2, u, halves[u])
+        for b in range(BLOCKS):
+            cols = slice(1024 * b, 1024 * (b + 1))
+            nc.vector.tensor_copy(
+                out=w4_w[:, :, cols].rearrange("p a (t q e) -> p a t q e", t=4, e=2),
+                in_=w4_raw_w[:, :, cols].rearrange("p a (q t e) -> p a t q e", t=4, e=2),
+            )
+        for a in range(BLOCKS):
+            for q in range(4):
+                nc.sync.dma_start(
+                    out=w4_s[32 * q : 32 * q + 4, a, :].bitcast(I32),
+                    in_=w4_dealt_s[16 * a + 4 * q : 16 * a + 4 * q + 4, :].bitcast(I32),
+                )
+        for t in range(4):
+            both_halves(banks0, 0, t, 2)
+
+        for t in range(2):
+            traits(banks0, 0, t)
+            read_panels(0, t, 0, M)
+        quantize_w1(1, 0, cast_w1(1, 0, False))
+        grouped11 = cast_w1(1, 1, True)
+        first_half = cast_w1_half(1, 2, 0, True)
+        quantize_w1(1, 1, grouped11)
+        quantize_w1_half(1, 2, 0, first_half)
+        for t in range(2, 4):
+            traits(banks0, 0, t)
+        second_half = cast_w1_half(1, 2, 1, False)
+        read_panels(0, 2, 0, M)
+        quantize_w1_half(1, 2, 1, second_half)
+        read_panels(0, 3, 0, M)
+        banks1 = [new_bank(i) for i in range(8)]
+        both_halves(banks1, 1, 0, 0)
+        both_halves(banks1, 1, 1, 0)
+        for t in range(4):
+            for a in range(1 if t < 2 else 0, PASSES1):
+                both_halves(banks1, 1, t, a)
+        respond(0, 0, 0, False)
+        respond(0, 1, 0, False)
+        traits(banks1, 1, 0)
+        read_panels(1, 0, 0, M)
+        traits(banks1, 1, 1)
+        read_panels(1, 1, 0, HALF)
+        respond(0, 2, 0, False)
+        traits(banks1, 1, 2)
+        read_panels(1, 2, 0, HALF)
+        respond(0, 3, 0, False)
+        traits(banks1, 1, 3)
+        quantize_z(0, 0, True)
+        read_panels(1, 3, 0, HALF)
+        respond(1, 0, 0, False)
+        respond(1, 1, 0, False)
+        read_panels(1, 1, HALF, M)
+        respond(1, 2, 0, True)
+        respond(1, 3, 0, True)
+        quantize_z(1, 0, True)
+        read_panels(1, 2, HALF, M)
+        read_panels(1, 3, HALF, M)
+        banks2 = [second_product(i, 0) for i in range(8)]
+        for i in range(8):
+            put_scores(banks2[i], i, 0)
+            if i < 4:
+                respond(i // 2, 2 * (i % 2), 1, False)
+                respond(i // 2, 2 * (i % 2) + 1, 1, False)
+            if i in (1, 3):
+                quantize_z(i // 2, 1, False)
+        for i in range(8):
+            put_scores(second_product(i, 1), i, 1)
+            nc.sync.dma_start(out=out_rows[i // 4, i % 4], in_=pages[i][:])

from contextlib import ExitStack

import concourse.mybir as mybir

K, H, N, T, S, M, T2 = 1536, 1024, 1024, 4096, 1024, 512, 1024
FLOPS = 2 * K * H * S + 2 * H * N * M

F32 = mybir.dt.float32
BF16 = mybir.dt.bfloat16
I32 = mybir.dt.int32
U32 = mybir.dt.uint32
U16 = mybir.dt.uint16
U8 = mybir.dt.uint8
FP8X4 = mybir.dt.float8_e4m3fn_x4
FP4X4 = mybir.dt.float4_e2m1fn_x4
ACT = mybir.ActivationFunctionType
MULT = mybir.AluOpType.mult

P = 128
BANK = 512
PASSES1 = K // 512
BLOCKS = H // 512
PAGES = 8
HALF = M // 2


def tile_list_larval_panel_scores_kernel(
    tc, tab_words, tab_scales, w1, w4_words, w4_scales, gain, shift, amp, wgt, wgo, offs, offs2, offs3, out
):
    nc = tc.nc
    with ExitStack() as ctx:
        keep = ctx.enter_context(tc.tile_pool(name="keep", bufs=1))
        ring = ctx.enter_context(tc.tile_pool(name="ring", bufs=1))
        psum = ctx.enter_context(tc.psum_pool(name="psum", bufs=1))

        list1 = keep.tile([P, S // 16], U16, name="list1")
        list2 = keep.tile([P, M // 16], U16, name="list2")
        list3 = keep.tile([P, M // 16], U16, name="list3")
        tab_w = [keep.tile([P, T], I32, name="tab_w%d" % a) for a in range(PASSES1)]
        tab_s = keep.tile([P, T], U8, name="tab_s")
        v_w = [keep.tile([P, S], U32, name="v_w%d" % a, align_bytes=64) for a in range(PASSES1)]
        v_s = keep.tile([P, S], U8, name="v_s", align_bytes=64)
        w1_raw = {}
        w1_w = {}
        w1_s = {}
        for b in range(BLOCKS):
            for a in range(PASSES1):
                w1_raw[b, a] = ring.tile([P, 4, 512], F32, name="w1_raw", tag="w1_raw", bufs=5)
                w1_w[b, a] = keep.tile([P, 512], U32, name="w1_w%d%d" % (b, a), align_bytes=64)
                w1_s[b, a] = keep.tile([P, 512], U8, name="w1_s%d%d" % (b, a), align_bytes=64)
        w4_raw_w = keep.tile([P, BLOCKS, 2 * N], U8, name="w4_raw_w")
        w4_raw_s = keep.tile([P, N], U8, name="w4_raw_s")
        w4_dealt_s = keep.tile([P, N], U8, name="w4_dealt_s")
        w4_w = keep.tile([P, BLOCKS, 2 * N], U8, name="w4_w", align_bytes=64)
        w4_s = keep.tile([P, BLOCKS, N], U8, name="w4_s", align_bytes=64)
        gain_t = keep.tile([P, BLOCKS, 4], F32, name="gain_t")
        shift_t = keep.tile([P, BLOCKS, 4], F32, name="shift_t")
        amp_t = keep.tile([P, BLOCKS, 4], F32, name="amp_t")
        wgt_t = keep.tile([P, M], F32, name="wgt_t")
        wgo_t = keep.tile([P, M], F32, name="wgo_t")
        pages = [keep.tile([P, T2], F32, name="page%d" % i) for i in range(PAGES)]
        z_w = [keep.tile([P, M], U32, name="z_w%d" % b, align_bytes=64) for b in range(BLOCKS)]
        z_s = [keep.tile([P, M], U8, name="z_s%d" % b, align_bytes=64) for b in range(BLOCKS)]

        def load_w1(b, a):
            rows = w1[512 * a : 512 * (a + 1), 512 * b : 512 * (b + 1)]
            nc.sync.dma_start(out=w1_raw[b, a][:], in_=rows.rearrange("(p j) c -> p j c", j=4))

        def load_table(a):
            nc.sync.dma_start(out=tab_w[a][:], in_=tab_words[a].rearrange("p t i -> p (t i)").bitcast(I32))

        def load_rows(dst, vec):
            nc.sync.dma_start(out=dst[:], in_=vec.rearrange("(b p i) -> p b i", b=BLOCKS, i=4))

        warm = keep.tile([P, 2], F32, name="warm")
        nc.vector.memset(warm[:], 0.0)
        nc.scalar.activation(out=warm[:, 1:2], in_=warm[:, 0:1], func=ACT.Silu)
        nc.vector.memset(tab_s[:].bitcast(I32), 0)
        nc.vector.memset(w4_raw_s[:].bitcast(I32), 0)
        nc.vector.memset(w4_s[:].bitcast(I32), 0)
        for page in pages:
            nc.vector.memset(page[:], 0.0)

        nc.sync.dma_start(list1[:], offs)
        load_table(0)
        for q in range(4):
            nc.sync.dma_start(
                out=tab_s[32 * q : 32 * q + 4 * PASSES1, :].bitcast(I32),
                in_=tab_scales[:, 4 * q : 4 * q + 4, :].bitcast(I32),
            )
        load_w1(0, 0)
        nc.sync.dma_start(
            out=w4_raw_s[0:32, :].bitcast(I32), in_=w4_scales.rearrange("a q n -> (a q) n").bitcast(I32)
        )
        load_w1(0, 1)
        load_table(1)
        load_table(2)
        load_w1(0, 2)
        nc.sync.dma_start(out=w4_raw_w[:].bitcast(I32), in_=w4_words.rearrange("a p n -> p a n").bitcast(I32))
        nc.sync.dma_start(out=wgt_t[:], in_=wgt)
        nc.sync.dma_start(list2[:], offs2)
        load_w1(1, 0)
        load_w1(1, 1)
        load_w1(1, 2)
        load_rows(gain_t, gain)
        load_rows(shift_t, shift)
        load_rows(amp_t, amp)
        nc.sync.dma_start(list3[:], offs3)
        nc.sync.dma_start(out=wgo_t[:], in_=wgo)

        def copy_on(on_vector, dst, src):
            if on_vector:
                nc.vector.tensor_copy(out=dst, in_=src)
            else:
                nc.scalar.copy(out=dst, in_=src)

        def cast_w1(b, a, on_vector):
            grouped = ring.tile([P, 2048], BF16, name="grouped", tag="grouped", bufs=2, align_bytes=64)
            dst = grouped[:].rearrange("p (t m j) -> p m j t", t=4, j=4)
            copy_on(on_vector, dst, w1_raw[b, a][:].rearrange("p j (m t) -> p m j t", t=4))
            return grouped

        def quantize_w1(b, a, grouped):
            nc.vector.quantize_mx(out=w1_w[b, a][:].bitcast(FP8X4), scales=w1_s[b, a][:], in_=grouped[:])

        def cast_w1_half(b, a, u, on_vector):
            grouped = ring.tile([P, 1024], BF16, name="grouped_half", tag="grouped_half", bufs=3, align_bytes=64)
            dst = grouped[:].rearrange("p (t m j) -> p m j t", t=2, j=4)
            src = w1_raw[b, a][:].rearrange("p j (m t) -> p m j t", t=4)
            copy_on(on_vector, dst, src[:, :, :, 2 * u : 2 * u + 2])
            return grouped

        def quantize_w1_half(b, a, u, grouped):
            cols = slice(256 * u, 256 * (u + 1))
            nc.vector.quantize_mx(out=w1_w[b, a][:, cols].bitcast(FP8X4), scales=w1_s[b, a][:, cols], in_=grouped[:])

        def gather_words(a, lo, hi):
            window = tab_w[a][:].bitcast(U32)
            nc.vector.tensor_copy(out=v_w[a][:, lo:hi], in_=window.indirect(list1[:, lo // 16 : hi // 16]))

        def new_bank(i):
            return psum.tile([P, BANK], F32, name="bank%d" % i, tag="bank%d" % i)

        def first_product(bank, b, t, half, a, order):
            cols = slice(128 * t, 128 * (t + 1))
            picks = slice(BANK * half, BANK * (half + 1))
            nc.tensor.matmul_mx(
                out=bank[:],
                lhsT=w1_w[b, a][:, cols].bitcast(FP8X4),
                lhsT_scale=w1_s[b, a][:, cols],
                rhs=v_w[a][:, picks].bitcast(FP8X4),
                rhs_scale=v_s[4 * a : P, picks],
                start=(a == order[0]),
                stop=(a == order[-1]),
            )

        def both_halves(banks, b, t, a):
            for half in range(2):
                first_product(banks[2 * t + half], b, t, half, a, (0, 1, 2))

        hs = {}
        xs = {}
        z_rows = {}
        for b in range(BLOCKS):
            for u in range(2):
                z_rows[b, u] = keep.tile([P, 4, HALF], BF16, name="z_rows%d%d" % (b, u))
            for t in range(4):
                xs[b, t] = keep.tile([P, M], F32, name="x%d%d" % (b, t))

        def traits(banks, b, t):
            h = ring.tile([P, S], F32, name="h", tag="h", bufs=4)
            for half in range(2):
                nc.scalar.activation(
                    out=h[:, BANK * half : BANK * (half + 1)], in_=banks[2 * t + half][:], func=ACT.Tanh
                )
            hs[b, t] = h

        def read_panels(b, t, lo, hi):
            window = hs[b, t][:].indirect(list2[:, lo // 16 : hi // 16])
            nc.vector.tensor_tensor(xs[b, t][:, lo:hi], window, wgt_t[:, lo:hi], MULT)

        def respond(b, t, u, on_vector):
            s = ring.tile([P, HALF], F32, name="s", tag="s", bufs=3)
            nc.scalar.activation(
                out=s[:],
                in_=xs[b, t][:, HALF * u : HALF * (u + 1)],
                func=ACT.Sin,
                bias=shift_t[:, b, t : t + 1],
                scale=gain_t[:, b, t : t + 1],
            )
            if on_vector:
                nc.vector.tensor_scalar(z_rows[b, u][:, t, :], s[:], amp_t[:, b, t : t + 1], None, MULT)
            else:
                nc.scalar.activation(out=z_rows[b, u][:, t, :], in_=s[:], func=ACT.Copy, scale=amp_t[:, b, t : t + 1])

        def quantize_z(b, u, on_vector):
            grouped = ring.tile([P, 1024], BF16, name="grouped_half", tag="grouped_half", bufs=3, align_bytes=64)
            copy_on(
                on_vector,
                grouped[:].rearrange("p (c e t) -> p c t e", e=4, t=4),
                z_rows[b, u][:].rearrange("p t (c e) -> p c t e", e=4),
            )
            cols = slice(HALF * u, HALF * (u + 1))
            nc.vector.quantize_mx(out=z_w[b][:, cols].bitcast(FP8X4), scales=z_s[b][:, cols], in_=grouped[:])

        out_rows = out.rearrange("(b p t) c -> b t p c", p=P, t=4)

        def second_product(i, u):
            bank = new_bank(i)
            for g in range(HALF // 128):
                cols = slice(HALF * u + 128 * g, HALF * u + 128 * (g + 1))
                for a in range(BLOCKS):
                    nc.tensor.matmul_mx(
                        out=bank[:, 128 * g : 128 * (g + 1)],
                        lhsT=w4_w[:, a, 256 * i : 256 * (i + 1)].bitcast(FP4X4),
                        lhsT_scale=w4_s[:, a, 128 * i : 128 * (i + 1)],
                        rhs=z_w[a][:, cols].bitcast(FP8X4),
                        rhs_scale=z_s[a][:, cols],
                        start=(a == 0),
                        stop=(a == BLOCKS - 1),
                    )
            return bank

        def put_scores(bank, i, u):
            y = ring.tile([P, HALF], F32, name="y", tag="y", bufs=4)
            nc.scalar.activation(out=y[:], in_=bank[:, 0:HALF], func=ACT.Abs)
            cols = slice(HALF * u, HALF * (u + 1))
            slots = pages[i][:].indirect(list3[:, HALF * u // 16 : HALF * (u + 1) // 16])
            nc.vector.tensor_tensor(slots, y[:], wgo_t[:, cols], MULT)

        gather_words(0, 0, S)
        nc.vector.tensor_copy(out=v_s[:], in_=tab_s[:].indirect(list1[:]))
        quantize_w1(0, 0, cast_w1(0, 0, False))
        banks0 = [new_bank(i) for i in range(8)]
        for t in range(4):
            both_halves(banks0, 0, t, 0)
        nc.vector.tensor_copy(
            out=w4_dealt_s[:].rearrange("p (b t q) -> p b t q", b=2, t=4),
            in_=w4_raw_s[:].rearrange("p (b q t) -> p b t q", b=2, t=4),
        )
        quantize_w1(0, 1, cast_w1(0, 1, False))
        gather_words(1, 0, S)
        for t in range(4):
            both_halves(banks0, 0, t, 1)
        gather_words(2, 0, S)
        halves = [cast_w1_half(0, 2, u, u == 0) for u in range(2)]
        for u in range(2):
            quantize_w1_half(0, 2, u, halves[u])
        for b in range(BLOCKS):
            cols = slice(1024 * b, 1024 * (b + 1))
            nc.vector.tensor_copy(
                out=w4_w[:, :, cols].rearrange("p a (t q e) -> p a t q e", t=4, e=2),
                in_=w4_raw_w[:, :, cols].rearrange("p a (q t e) -> p a t q e", t=4, e=2),
            )
        for a in range(BLOCKS):
            for q in range(4):
                nc.sync.dma_start(
                    out=w4_s[32 * q : 32 * q + 4, a, :].bitcast(I32),
                    in_=w4_dealt_s[16 * a + 4 * q : 16 * a + 4 * q + 4, :].bitcast(I32),
                )
        for t in range(4):
            both_halves(banks0, 0, t, 2)

        for t in range(2):
            traits(banks0, 0, t)
            read_panels(0, t, 0, M)
        quantize_w1(1, 0, cast_w1(1, 0, False))
        grouped11 = cast_w1(1, 1, True)
        first_half = cast_w1_half(1, 2, 0, True)
        quantize_w1(1, 1, grouped11)
        quantize_w1_half(1, 2, 0, first_half)
        for t in range(2, 4):
            traits(banks0, 0, t)
        second_half = cast_w1_half(1, 2, 1, False)
        read_panels(0, 2, 0, M)
        quantize_w1_half(1, 2, 1, second_half)
        read_panels(0, 3, 0, M)
        banks1 = [new_bank(i) for i in range(8)]
        both_halves(banks1, 1, 0, 0)
        both_halves(banks1, 1, 1, 0)
        for t in range(4):
            for a in range(1 if t < 2 else 0, PASSES1):
                both_halves(banks1, 1, t, a)
        respond(0, 0, 0, False)
        respond(0, 1, 0, False)
        traits(banks1, 1, 0)
        read_panels(1, 0, 0, M)
        traits(banks1, 1, 1)
        read_panels(1, 1, 0, HALF)
        respond(0, 2, 0, False)
        traits(banks1, 1, 2)
        read_panels(1, 2, 0, HALF)
        respond(0, 3, 0, False)
        traits(banks1, 1, 3)
        quantize_z(0, 0, True)
        read_panels(1, 3, 0, HALF)
        respond(1, 0, 0, False)
        respond(1, 1, 0, False)
        read_panels(1, 1, HALF, M)
        respond(1, 2, 0, True)
        respond(1, 3, 0, True)
        quantize_z(1, 0, True)
        read_panels(1, 2, HALF, M)
        read_panels(1, 3, HALF, M)
        banks2 = [second_product(i, 0) for i in range(8)]
        for i in range(8):
            put_scores(banks2[i], i, 0)
            if i < 4:
                respond(i // 2, 2 * (i % 2), 1, False)
                respond(i // 2, 2 * (i % 2) + 1, 1, False)
            if i in (1, 3):
                quantize_z(i // 2, 1, False)
        for i in range(8):
            put_scores(second_product(i, 1), i, 1)
            nc.sync.dma_start(out=out_rows[i // 4, i % 4], in_=pages[i][:])
